import numpy as np
import ml_dtypes


def mxq(x, axis, fmt="e4m3"):
    dtype, down = {"e4m3": (ml_dtypes.float8_e4m3fn, 7), "e5m2": (ml_dtypes.float8_e5m2, 14)}[fmt]
    v = np.moveaxis(np.asarray(x, np.float32).astype(ml_dtypes.bfloat16).astype(np.float64), axis, -1)
    blocks = v.reshape(v.shape[:-1] + (-1, 32))
    amax = np.abs(blocks).max(-1, keepdims=True)
    byte = np.maximum(np.where(amax > 0, np.frexp(amax)[1] - 1 + 127, 0) - down, 1)
    scale = np.exp2(byte - 127.0)
    codes = (blocks / scale).astype(np.float32).astype(dtype).astype(np.float64)
    return np.moveaxis((codes * scale).reshape(v.shape), -1, axis)


WIDE = False


def mx_kscale(k):
    if not WIDE:
        return np.ones(k)
    levels = np.array([10, -10, 5, -5, 0])
    if k % 512:
        return np.exp2(np.random.permutation(np.resize(levels, k // 32))).repeat(32)
    a = np.empty((k // 512, 16))
    for p in range(k // 512):
        a[p, :8] = np.random.permutation(np.resize(levels, 8))
        for g in range(8):
            far = levels[np.abs(levels - a[p, g]) >= 10]
            a[p, g + 8] = far[np.random.randint(len(far))]
    return np.exp2(a.ravel()).repeat(32)


def f64(x):
    return np.asarray(x).astype(np.float64)


def striped(idx):
    return np.tile(idx.reshape(-1, 16).T, (8, 1)).astype(np.uint16)


def unstriped(offs):
    return offs[:16].T.reshape(-1).astype(np.int64)


def striped8(idx):
    return np.concatenate([x.reshape(-1, 16).T for x in idx]).astype(np.uint16)


def runs(offs, k):
    lists = np.stack([offs[16 * r : 16 * r + 16].T.reshape(-1) for r in range(8)]).astype(np.int64)
    return lists[np.arange(k) % 512 // 64]


def pack_weight(w):
    k, n = w.shape
    w = f64(np.asarray(w, np.float32).astype(ml_dtypes.bfloat16)).reshape(k // 32, 32, n)
    amax = np.abs(w).max(1)
    byte = np.clip(np.where(amax > 0, np.frexp(amax)[1] - 1 + 127 - 7, 1), 1, 254)
    scaled = (w * np.exp2(127.0 - byte)[:, None, :]).reshape(k, n).astype(np.float32)
    words = np.ascontiguousarray(scaled.reshape(k // 512, 128, 4, n).transpose(0, 1, 3, 2)).astype(ml_dtypes.float8_e4m3fn).view(np.uint8)
    return words, np.ascontiguousarray(byte.astype(np.uint8).reshape(k // 512, 16, n))


def unpack_weight(words, scales):
    g, p, n, _ = words.shape
    vals = np.ascontiguousarray(words).view(ml_dtypes.float8_e4m3fn).astype(np.float64) * np.repeat(np.exp2(scales.astype(np.float64) - 127.0), 8, axis=1)[..., None]
    return vals.transpose(0, 1, 3, 2).reshape(g * 512, n)

def planes(y):
    n, m = y.shape
    v = y.astype(np.float32).astype(ml_dtypes.bfloat16).astype(np.float64).reshape(n // 32, 32, m)
    top = np.abs(v).max(1)
    byte = np.clip(np.where(top > 0, np.frexp(top)[1] - 1 + 127 - 7, 1), 1, 254)
    codes = (v * np.exp2(127.0 - byte)[:, None, :]).reshape(n, m).astype(np.float32).astype(ml_dtypes.float8_e4m3fn).view(np.uint8)
    words = codes.reshape(n // 512, 128, 4, m).transpose(0, 1, 3, 2)
    return np.ascontiguousarray(words), np.ascontiguousarray(byte.astype(np.uint8).reshape(n // 512, 16, m))


K, T, S, G, H, W = 512, 1024, 256, 2048, 512, 128


def setup_inputs():
    n = np.random.standard_normal
    s = mx_kscale(K)[:, None]
    packed_xT = pack_weight(n((K, T)) * s)
    packed_dT = pack_weight(n((K, G)) / s)
    perm = np.random.permutation(S)
    return {
        "x_words": packed_xT[0],
        "x_scales": packed_xT[1],
        "d_words": packed_dT[0],
        "d_scales": packed_dT[1],
        "gs": (np.random.uniform(0.5, 1.5, (K, 1)) * s).astype(np.float32),
        "offs": striped8(np.random.randint(0, T, (8, S))),
        "k1": striped8(np.random.randint(0, G, (8, H))),
        "n1": striped(np.random.permutation(S)),
        "k2": striped8(np.random.randint(0, G, (8, H))),
        "n2": striped(perm[:W]),
        "n3": striped(perm[W:]),
    }


def reference(x_words, x_scales, d_words, d_scales, gs, offs, k1, n1, k2, n2, n3):
    d_k2 = unpack_weight(d_words, d_scales)[np.arange(K)[:, None], runs(k2, K)]
    d_k1 = unpack_weight(d_words, d_scales)[np.arange(K)[:, None], runs(k1, K)]
    xq = unpack_weight(x_words, x_scales)[np.arange(K)[:, None], runs(offs, K)]
    h = 0.0625 * (d_k1.T @ xq)
    ds = np.zeros((H, S))
    ds[:, unstriped(n1)] = h
    z = f64(gs) * (h - ds)
    h2 = 0.0625 * ((d_k2.T @ mxq(z, 0, "e4m3")))
    pb = h2[:, unstriped(n3)]
    pa = h2[:, unstriped(n2)]
    rb = pb - (0.5 * pa)
    ra = np.sqrt((pa) ** 2 + (pb) ** 2 + 0.25)
    ds2 = np.zeros((H, S))
    ds2[:, unstriped(n2)] = ra
    out = ds2.copy()
    out[:, unstriped(n3)] = rb
    return (out,) + planes(out)

@@ -1,0 +1,235 @@
+from contextlib import ExitStack
+
+import concourse.mybir as mybir
+
+K, T, S, G, H, W = 512, 1024, 256, 2048, 512, 128
+FLOPS = 2 * (2 * K * H * S)
+
+F32 = mybir.dt.float32
+BF16 = mybir.dt.bfloat16
+I32 = mybir.dt.int32
+U32 = mybir.dt.uint32
+U16 = mybir.dt.uint16
+U8 = mybir.dt.uint8
+FP8X4 = mybir.dt.float8_e4m3fn_x4
+ALU = mybir.AluOpType
+ACT = mybir.ActivationFunctionType
+
+P = 128
+PACK = 4
+HALF = S // 2
+SIXTEENTH = 0.0625
+LEAD = 512
+
+
+def tile_picked_hcodesendmxpolar_none_po_kernel(
+    tc, x_words, x_scales, d_words, d_scales, gs, offs, k1, n1, k2, n2, n3, out_0, out_1, out_2
+):
+    nc = tc.nc
+    with ExitStack() as ctx:
+        keep = ctx.enter_context(tc.tile_pool(name="keep", bufs=1))
+        psum = ctx.enter_context(tc.psum_pool(name="psum", bufs=1))
+
+        def sbuf(name, shape, dtype, tag=""):
+            return keep.tile(shape, dtype, name=name, tag=tag, align_bytes=64)
+
+        def load_list(name, dram):
+            tile = sbuf(name, list(dram.shape), U16)
+            nc.sync.dma_start(tile[:], dram)
+            return tile
+
+        def move_scale_rows(dst, src, queues):
+            for a in range(PACK):
+                queues[a].dma_start(dst[a:P:32, :].bitcast(I32), src[8 * a : P : 32, :].bitcast(I32))
+
+        d_bytes = sbuf("d_bytes", [P, G], U8)
+        x_bytes = sbuf("x_bytes", [P, T], U8)
+        placed1 = sbuf("placed1", [P, H + S], U8, tag="placed1_then_words2")
+        placed2 = sbuf("placed2", [P, H], U8, tag="placed2_then_z")
+        nc.vector.memset(d_bytes[:].bitcast(I32), 0)
+        nc.vector.memset(x_bytes[:].bitcast(I32), 0)
+        nc.vector.memset(placed1[:].bitcast(I32), 0)
+        nc.vector.memset(placed2[:].bitcast(I32), 0)
+
+        d_table = sbuf("d_table", [P, G], U32)
+        x_table = sbuf("x_table", [P, T], U32)
+        d_rows = d_words[0].rearrange("p c r -> p (c r)").bitcast(I32)
+        k1_list = load_list("k1_list", k1)
+        nc.sync.dma_start(d_table[:, :LEAD].bitcast(I32), d_rows[:, :LEAD])
+        offs_list = load_list("offs_list", offs)
+        k2_list = load_list("k2_list", k2)
+        n1_list = load_list("n1_list", n1)
+        nc.sync.dma_start(d_bytes[0:P:8, :].bitcast(I32), d_scales[0].bitcast(I32))
+        nc.sync.dma_start(x_bytes[0:P:8, :].bitcast(I32), x_scales[0].bitcast(I32))
+        nc.sync.dma_start(d_table[:, LEAD:].bitcast(I32), d_rows[:, LEAD:])
+        nc.sync.dma_start(x_table[:].bitcast(I32), x_words[0].rearrange("p c r -> p (c r)").bitcast(I32))
+        n2_list = load_list("n2_list", n2)
+        n3_list = load_list("n3_list", n3)
+        gain = sbuf("gain", [P, PACK], F32)
+        nc.gpsimd.dma_start(gain[:], gs.rearrange("(p t) o -> p (t o)", t=PACK))
+
+        picked_bytes1 = sbuf("picked_bytes1", [P, H + S], U8, tag="bytes1_words1_bytes2")
+        nc.vector.tensor_copy(picked_bytes1[:, :H], d_bytes[:].indirect(k1_list[:]))
+        nc.vector.tensor_copy(picked_bytes1[:, H:], x_bytes[:].indirect(offs_list[:]))
+        move_scale_rows(placed1, picked_bytes1, [nc.sync, nc.scalar, nc.sync, nc.scalar])
+
+        picked_words1 = sbuf("picked_words1", [P, H], U32)
+        x_picked = sbuf("x_picked", [P, S], U32)
+        nc.vector.tensor_copy(picked_words1[:], d_table[:].indirect(k1_list[:]))
+        nc.vector.tensor_copy(x_picked[:], x_table[:].indirect(offs_list[:]))
+
+        def deal(dst, src, line, first, count):
+            nc.vector.tensor_copy(
+                dst.rearrange("p (t c i) -> p c t i", t=count, i=line),
+                src.rearrange("p (c i t) -> p c t i", t=PACK, i=line)[:, :, first : first + count, :],
+            )
+
+        words1_first = sbuf("words1_first", [P, P], U32)
+        bytes1 = sbuf("bytes1", [P, H], U8, tag="dealt_bytes1_then_z_rows")
+        deal(words1_first[:], picked_words1[:], 4, 0, 1)
+        deal(bytes1[:, :P], placed1[:, :H], 16, 0, 1)
+
+        def product(name, words, scale_bytes, moving, moving_bytes):
+            bank = psum.tile([P, S], F32, name=name)
+            nc.tensor.matmul_mx(
+                out=bank[:],
+                lhsT=words.bitcast(FP8X4),
+                lhsT_scale=scale_bytes,
+                rhs=moving.bitcast(FP8X4),
+                rhs_scale=moving_bytes,
+                start=True,
+                stop=True,
+            )
+            return bank
+
+        hidden = []
+        sent = []
+
+        banks = []
+
+        def first_product(t, words):
+            banks.append(product("first%d" % t, words, bytes1[:, t * P : (t + 1) * P], x_picked[:], placed1[:, H:]))
+
+        def first_layer(t):
+            bank = banks[t]
+            hidden.append(sbuf("hidden%d" % t, [P, S], F32))
+            nc.vector.tensor_scalar(hidden[t][:], bank[:], gain[:, t : t + 1], SIXTEENTH, ALU.mult, ALU.mult)
+            sent.append(sbuf("sent%d" % t, [P, 2 * S], F32))
+            nc.scalar.activation(sent[t][:].indirect(n1_list[:]), hidden[t][:], ACT.Copy)
+
+        first_product(0, words1_first[:])
+        first_layer(0)
+        words1_rest = sbuf("words1_rest", [P, H - P], U32, tag="bytes1_words1_bytes2")
+        deal(words1_rest[:], picked_words1[:], 4, 1, PACK - 1)
+        deal(bytes1[:, P:], placed1[:, :H], 16, 1, PACK - 1)
+        for t in range(1, PACK):
+            first_product(t, words1_rest[:, (t - 1) * P : t * P])
+        first_layer(1)
+
+        picked_bytes2 = sbuf("picked_bytes2", [P, H], U8, tag="bytes1_words1_bytes2")
+        nc.vector.tensor_copy(picked_bytes2[:], d_bytes[:].indirect(k2_list[:]))
+        move_scale_rows(placed2, picked_bytes2, [nc.sync] * PACK)
+        first_layer(2)
+        first_layer(3)
+
+        picked_words2 = sbuf("picked_words2", [P, H], U32, tag="placed1_then_words2")
+        nc.vector.tensor_copy(picked_words2[:], d_table[:].indirect(k2_list[:]))
+        words2 = sbuf("words2", [P, H], U32)
+        bytes2 = sbuf("bytes2", [P, H], U8)
+        z_rows = sbuf("z_rows", [P, PACK - 1, S], BF16, tag="dealt_bytes1_then_z_rows")
+        for t in range(PACK - 2):
+            nc.vector.tensor_tensor(z_rows[:, t, :], hidden[t][:], sent[t][:, :S], ALU.subtract)
+        deal(words2[:], picked_words2[:], 4, 0, PACK)
+        deal(bytes2[:], placed2[:], 16, 0, PACK)
+        t = PACK - 2
+        nc.vector.tensor_tensor(z_rows[:, t, :], hidden[t][:], sent[t][:, :S], ALU.subtract)
+
+        halves = [slice(0, HALF), slice(HALF, S)]
+        z_tile = sbuf("z_tile", [P, S * PACK], BF16, tag="placed2_then_z")
+        z_flat = [z_tile[:, u * HALF * PACK : (u + 1) * HALF * PACK] for u in range(2)]
+        z_grouped = [z_flat[u].rearrange("p (c t) -> p c t", t=PACK) for u in range(2)]
+        for u in range(2):
+            nc.vector.tensor_copy(z_grouped[u][:, :, : PACK - 1], z_rows[:, :, halves[u]].rearrange("p t c -> p c t"))
+        t = PACK - 1
+        for u in range(2):
+            nc.vector.tensor_tensor(z_grouped[u][:, :, t], hidden[t][:, halves[u]], sent[t][:, halves[u]], ALU.subtract)
+        z_words = sbuf("z_words", [P, S], U32)
+        z_bytes = sbuf("z_bytes", [P, S], U8)
+        for u in range(2):
+            nc.vector.quantize_mx(
+                out=z_words[:, halves[u]].bitcast(FP8X4),
+                scales=z_bytes[:, halves[u]],
+                in_=z_flat[u],
+            )
+
+        pairs, rb, radicand, ra, result = [], [], [], [], []
+        out_rows = out_0.rearrange("(p t) s -> p t s", t=PACK)
+
+        def fetch(t):
+            bank = product("second%d" % t, words2[:, t * P : (t + 1) * P], bytes2[:, t * P : (t + 1) * P], z_words[:], z_bytes[:])
+            h2 = sbuf("h2_%d" % t, [P, S], F32)
+            nc.vector.tensor_scalar(h2[:], bank[:], SIXTEENTH, None, ALU.mult)
+            pairs.append(sbuf("pairs%d" % t, [P, 2 * W], F32, tag="pairs%d" % t))
+            nc.scalar.activation(pairs[t][:, :W], h2[:].indirect(n2_list[:]), ACT.Copy)
+            nc.scalar.activation(pairs[t][:, W:], h2[:].indirect(n3_list[:]), ACT.Copy)
+
+        def combine(t):
+            rb.append(sbuf("rb%d" % t, [P, W], F32))
+            nc.vector.scalar_tensor_tensor(rb[t][:], pairs[t][:, :W], -0.5, pairs[t][:, W:], ALU.mult, ALU.add)
+            squares = sbuf("squares%d" % t, [P, 2 * W], F32, tag="squares%d" % t)
+            nc.vector.tensor_tensor(squares[:], pairs[t][:], pairs[t][:], ALU.mult)
+            radicand.append(sbuf("radicand%d" % t, [P, W], F32))
+            nc.vector.scalar_tensor_tensor(radicand[t][:], squares[:, :W], 0.25, squares[:, W:], ALU.add, ALU.add)
+
+        def put_rb(t):
+            result.append(sbuf("result%d" % t, [P, S], F32))
+            nc.scalar.activation(result[t][:].indirect(n3_list[:]), rb[t][:], ACT.Copy)
+
+        def root(t):
+            ra.append(sbuf("ra%d" % t, [P, W], F32))
+            nc.scalar.activation(ra[t][:], radicand[t][:], ACT.Sqrt)
+
+        def put_ra(t):
+            nc.scalar.activation(result[t][:].indirect(n2_list[:]), ra[t][:], ACT.Copy)
+            nc.sync.dma_start(out_rows[:, t, :], result[t][:])
+
+        fetch(0)
+        fetch(1)
+        combine(0)
+        put_rb(0)
+        root(0)
+        fetch(2)
+        combine(1)
+        put_ra(0)
+        root(1)
+        put_rb(1)
+        fetch(3)
+        combine(2)
+        put_ra(1)
+        root(2)
+        put_rb(2)
+        combine(3)
+        root(3)
+        put_rb(3)
+        put_ra(2)
+        put_ra(3)
+
+        reused = ["pairs%d" % (PACK - 1), "squares%d" % (PACK - 1)]
+        out_grouped = [sbuf("out_grouped%d" % u, [P, HALF, PACK], BF16, tag=reused[u]) for u in range(2)]
+        for t in range(PACK):
+            for u in range(2):
+                nc.vector.tensor_copy(out_grouped[u][:, :, t], result[t][:, halves[u]])
+
+        out_words = sbuf("out_words", [P, S], U32)
+        out_bytes = sbuf("out_bytes", [P, S], U8)
+        for u in range(2):
+            nc.vector.quantize_mx(
+                out=out_words[:, halves[u]].bitcast(FP8X4),
+                scales=out_bytes[:, halves[u]],
+                in_=out_grouped[u][:].rearrange("p c t -> p (c t)"),
+            )
+        nc.sync.dma_start(out_1[0].rearrange("p c r -> p (c r)").bitcast(I32), out_words[:].bitcast(I32))
+        scale_rows = out_2[0].bitcast(I32)
+        for q in range(4):
+            queue = nc.scalar if q % 2 == 0 else nc.sync
+            queue.dma_start(scale_rows[4 * q : 4 * q + 4, :], out_bytes[32 * q : 32 * q + 4, :].bitcast(I32))

@@ -51,6 +51,10 @@ def tile_picked_hcodesendmxpolar_none_po_kernel(
         nc.vector.memset(placed1[:].bitcast(I32), 0)
         nc.vector.memset(placed2[:].bitcast(I32), 0)
 
+        warm = sbuf("warm", [P, 2], F32)
+        nc.gpsimd.memset(warm[:, 0:1], 1.0)
+        nc.scalar.activation(warm[:, 1:2], warm[:, 0:1], ACT.Sqrt)
+
         d_table = sbuf("d_table", [P, G], U32)
         x_table = sbuf("x_table", [P, T], U32)
         d_rows = d_words[0].rearrange("p c r -> p (c r)").bitcast(I32)

@@ -46,8 +46,8 @@ def tile_picked_hcodesendmxpolar_none_po_kernel(
         x_bytes = sbuf("x_bytes", [P, T], U8)
         placed1 = sbuf("placed1", [P, H + S], U8, tag="placed1_then_words2")
         placed2 = sbuf("placed2", [P, H], U8, tag="placed2_then_z")
-        nc.vector.memset(d_bytes[:].bitcast(I32), 0)
         nc.vector.memset(x_bytes[:].bitcast(I32), 0)
+        nc.vector.memset(d_bytes[:].bitcast(I32), 0)
         nc.vector.memset(placed1[:].bitcast(I32), 0)
         nc.vector.memset(placed2[:].bitcast(I32), 0)
 
@@ -58,13 +58,13 @@ def tile_picked_hcodesendmxpolar_none_po_kernel(
         d_table = sbuf("d_table", [P, G], U32)
         x_table = sbuf("x_table", [P, T], U32)
         d_rows = d_words[0].rearrange("p c r -> p (c r)").bitcast(I32)
+        offs_list = load_list("offs_list", offs)
         k1_list = load_list("k1_list", k1)
         nc.sync.dma_start(d_table[:, :LEAD].bitcast(I32), d_rows[:, :LEAD])
-        offs_list = load_list("offs_list", offs)
+        nc.sync.dma_start(x_bytes[0:P:8, :].bitcast(I32), x_scales[0].bitcast(I32))
+        nc.sync.dma_start(d_bytes[0:P:8, :].bitcast(I32), d_scales[0].bitcast(I32))
         k2_list = load_list("k2_list", k2)
         n1_list = load_list("n1_list", n1)
-        nc.sync.dma_start(d_bytes[0:P:8, :].bitcast(I32), d_scales[0].bitcast(I32))
-        nc.sync.dma_start(x_bytes[0:P:8, :].bitcast(I32), x_scales[0].bitcast(I32))
         nc.sync.dma_start(d_table[:, LEAD:].bitcast(I32), d_rows[:, LEAD:])
         nc.sync.dma_start(x_table[:].bitcast(I32), x_words[0].rearrange("p c r -> p (c r)").bitcast(I32))
         n2_list = load_list("n2_list", n2)
@@ -73,8 +73,8 @@ def tile_picked_hcodesendmxpolar_none_po_kernel(
         nc.gpsimd.dma_start(gain[:], gs.rearrange("(p t) o -> p (t o)", t=PACK))
 
         picked_bytes1 = sbuf("picked_bytes1", [P, H + S], U8, tag="bytes1_words1_bytes2")
-        nc.vector.tensor_copy(picked_bytes1[:, :H], d_bytes[:].indirect(k1_list[:]))
         nc.vector.tensor_copy(picked_bytes1[:, H:], x_bytes[:].indirect(offs_list[:]))
+        nc.vector.tensor_copy(picked_bytes1[:, :H], d_bytes[:].indirect(k1_list[:]))
         move_scale_rows(placed1, picked_bytes1, [nc.sync, nc.scalar, nc.sync, nc.scalar])
 
         picked_words1 = sbuf("picked_words1", [P, H], U32)
@@ -93,8 +93,8 @@ def tile_picked_hcodesendmxpolar_none_po_kernel(
         deal(words1_first[:], picked_words1[:], 4, 0, 1)
         deal(bytes1[:, :P], placed1[:, :H], 16, 0, 1)
 
-        def product(name, words, scale_bytes, moving, moving_bytes):
-            bank = psum.tile([P, S], F32, name=name)
+        def product(name, tag, words, scale_bytes, moving, moving_bytes):
+            bank = psum.tile([P, moving.shape[1]], F32, name=name, tag=tag)
             nc.tensor.matmul_mx(
                 out=bank[:],
                 lhsT=words.bitcast(FP8X4),
@@ -106,23 +106,31 @@ def tile_picked_hcodesendmxpolar_none_po_kernel(
             )
             return bank
 
-        hidden = []
+        hidden = [sbuf("hidden%d" % t, [P, S], F32) for t in range(PACK)]
         sent = []
 
-        banks = []
+        banks = {}
+        halves = [slice(0, HALF), slice(HALF, S)]
+        x_plane = placed1[:, H:]
 
         def first_product(t, words):
-            banks.append(product("first%d" % t, words, bytes1[:, t * P : (t + 1) * P], x_picked[:], placed1[:, H:]))
+            banks[t] = product("first%d" % t, "bank%d" % t, words, bytes1[:, t * P : (t + 1) * P], x_picked[:], x_plane)
 
-        def first_layer(t):
-            bank = banks[t]
-            hidden.append(sbuf("hidden%d" % t, [P, S], F32))
-            nc.vector.tensor_scalar(hidden[t][:], bank[:], gain[:, t : t + 1], SIXTEENTH, ALU.mult, ALU.mult)
-            sent.append(sbuf("sent%d" % t, [P, 2 * S], F32))
+        def weigh(t, bank, cols):
+            nc.vector.tensor_scalar(hidden[t][:, cols], bank[:], gain[:, t : t + 1], SIXTEENTH, ALU.mult, ALU.mult)
+
+        def send(t):
+            sent.append(sbuf("sent%d" % t, [P, 2 * S], F32, tag="sent%d" % t))
             nc.scalar.activation(sent[t][:].indirect(n1_list[:]), hidden[t][:], ACT.Copy)
 
-        first_product(0, words1_first[:])
-        first_layer(0)
+        def first_layer(t):
+            weigh(t, banks[t], slice(0, S))
+            send(t)
+
+        for u in range(2):
+            bank = product("first0_%d" % u, "bank%d" % (PACK + u), words1_first[:], bytes1[:, :P], x_picked[:, halves[u]], x_plane[:, halves[u]])
+            weigh(0, bank, halves[u])
+        send(0)
         words1_rest = sbuf("words1_rest", [P, H - P], U32, tag="bytes1_words1_bytes2")
         deal(words1_rest[:], picked_words1[:], 4, 1, PACK - 1)
         deal(bytes1[:, P:], placed1[:, :H], 16, 1, PACK - 1)
@@ -138,17 +146,16 @@ def tile_picked_hcodesendmxpolar_none_po_kernel(
 
         picked_words2 = sbuf("picked_words2", [P, H], U32, tag="placed1_then_words2")
         nc.vector.tensor_copy(picked_words2[:], d_table[:].indirect(k2_list[:]))
-        words2 = sbuf("words2", [P, H], U32)
+        words2_first = sbuf("words2_first", [P, 2 * P], U32)
         bytes2 = sbuf("bytes2", [P, H], U8)
         z_rows = sbuf("z_rows", [P, PACK - 1, S], BF16, tag="dealt_bytes1_then_z_rows")
         for t in range(PACK - 2):
             nc.vector.tensor_tensor(z_rows[:, t, :], hidden[t][:], sent[t][:, :S], ALU.subtract)
-        deal(words2[:], picked_words2[:], 4, 0, PACK)
+        deal(words2_first[:], picked_words2[:], 4, 0, 2)
         deal(bytes2[:], placed2[:], 16, 0, PACK)
         t = PACK - 2
         nc.vector.tensor_tensor(z_rows[:, t, :], hidden[t][:], sent[t][:, :S], ALU.subtract)
 
-        halves = [slice(0, HALF), slice(HALF, S)]
         z_tile = sbuf("z_tile", [P, S * PACK], BF16, tag="placed2_then_z")
         z_flat = [z_tile[:, u * HALF * PACK : (u + 1) * HALF * PACK] for u in range(2)]
         z_grouped = [z_flat[u].rearrange("p (c t) -> p c t", t=PACK) for u in range(2)]
@@ -166,13 +173,22 @@ def tile_picked_hcodesendmxpolar_none_po_kernel(
                 in_=z_flat[u],
             )
 
+        words2_rest = sbuf("words2_rest", [P, 2 * P], U32, tag="sent%d" % (PACK - 1))
+        deal(words2_rest[:], picked_words2[:], 4, 2, 2)
+        words2 = [tile[:, c * P : (c + 1) * P] for tile in (words2_first, words2_rest) for c in range(2)]
+
         pairs, rb, radicand, ra, result = [], [], [], [], []
         out_rows = out_0.rearrange("(p t) s -> p t s", t=PACK)
 
         def fetch(t):
-            bank = product("second%d" % t, words2[:, t * P : (t + 1) * P], bytes2[:, t * P : (t + 1) * P], z_words[:], z_bytes[:])
             h2 = sbuf("h2_%d" % t, [P, S], F32)
-            nc.vector.tensor_scalar(h2[:], bank[:], SIXTEENTH, None, ALU.mult)
+            if t == 0:
+                for u in range(2):
+                    bank = product("second0_%d" % u, "bank%d" % (PACK + u), words2[0], bytes2[:, :P], z_words[:, halves[u]], z_bytes[:, halves[u]])
+                    nc.scalar.activation(h2[:, halves[u]], bank[:], ACT.Copy, scale=SIXTEENTH)
+            else:
+                bank = product("second%d" % t, "bank%d" % t, words2[t], bytes2[:, t * P : (t + 1) * P], z_words[:], z_bytes[:])
+                nc.vector.tensor_scalar(h2[:], bank[:], SIXTEENTH, None, ALU.mult)
             pairs.append(sbuf("pairs%d" % t, [P, 2 * W], F32, tag="pairs%d" % t))
             nc.scalar.activation(pairs[t][:, :W], h2[:].indirect(n2_list[:]), ACT.Copy)
             nc.scalar.activation(pairs[t][:, W:], h2[:].indirect(n3_list[:]), ACT.Copy)
@@ -224,6 +240,7 @@ def tile_picked_hcodesendmxpolar_none_po_kernel(
             for u in range(2):
                 nc.vector.tensor_copy(out_grouped[u][:, :, t], result[t][:, halves[u]])
 
+        word_rows = out_1[0].rearrange("p c r -> p (c r)").bitcast(I32)
         out_words = sbuf("out_words", [P, S], U32)
         out_bytes = sbuf("out_bytes", [P, S], U8)
         for u in range(2):
@@ -232,7 +249,7 @@ def tile_picked_hcodesendmxpolar_none_po_kernel(
                 scales=out_bytes[:, halves[u]],
                 in_=out_grouped[u][:].rearrange("p c t -> p (c t)"),
             )
-        nc.sync.dma_start(out_1[0].rearrange("p c r -> p (c r)").bitcast(I32), out_words[:].bitcast(I32))
+            nc.sync.dma_start(word_rows[:, halves[u]], out_words[:, halves[u]].bitcast(I32))
         scale_rows = out_2[0].bitcast(I32)
         for q in range(4):
             queue = nc.scalar if q % 2 == 0 else nc.sync

@@ -19,7 +19,7 @@ P = 128
 PACK = 4
 HALF = S // 2
 SIXTEENTH = 0.0625
-LEAD = 512
+LEAD = 256
 
 
 def tile_picked_hcodesendmxpolar_none_po_kernel(
@@ -46,7 +46,7 @@ def tile_picked_hcodesendmxpolar_none_po_kernel(
         x_bytes = sbuf("x_bytes", [P, T], U8)
         placed1 = sbuf("placed1", [P, H + S], U8, tag="placed1_then_words2")
         placed2 = sbuf("placed2", [P, H], U8, tag="placed2_then_z")
-        nc.vector.memset(x_bytes[:].bitcast(I32), 0)
+        nc.gpsimd.memset(x_bytes[:].bitcast(I32), 0)
         nc.vector.memset(d_bytes[:].bitcast(I32), 0)
         nc.vector.memset(placed1[:].bitcast(I32), 0)
         nc.vector.memset(placed2[:].bitcast(I32), 0)
@@ -63,9 +63,9 @@ def tile_picked_hcodesendmxpolar_none_po_kernel(
         nc.sync.dma_start(d_table[:, :LEAD].bitcast(I32), d_rows[:, :LEAD])
         nc.sync.dma_start(x_bytes[0:P:8, :].bitcast(I32), x_scales[0].bitcast(I32))
         nc.sync.dma_start(d_bytes[0:P:8, :].bitcast(I32), d_scales[0].bitcast(I32))
+        nc.sync.dma_start(d_table[:, LEAD:].bitcast(I32), d_rows[:, LEAD:])
         k2_list = load_list("k2_list", k2)
         n1_list = load_list("n1_list", n1)
-        nc.sync.dma_start(d_table[:, LEAD:].bitcast(I32), d_rows[:, LEAD:])
         nc.sync.dma_start(x_table[:].bitcast(I32), x_words[0].rearrange("p c r -> p (c r)").bitcast(I32))
         n2_list = load_list("n2_list", n2)
         n3_list = load_list("n3_list", n3)

from contextlib import ExitStack

import concourse.mybir as mybir

K, T, S, G, H, W = 512, 1024, 256, 2048, 512, 128
FLOPS = 2 * (2 * K * H * S)

F32 = mybir.dt.float32
BF16 = mybir.dt.bfloat16
I32 = mybir.dt.int32
U32 = mybir.dt.uint32
U16 = mybir.dt.uint16
U8 = mybir.dt.uint8
FP8X4 = mybir.dt.float8_e4m3fn_x4
ALU = mybir.AluOpType
ACT = mybir.ActivationFunctionType

P = 128
PACK = 4
HALF = S // 2
SIXTEENTH = 0.0625
LEAD = 256


def tile_picked_hcodesendmxpolar_none_po_kernel(
    tc, x_words, x_scales, d_words, d_scales, gs, offs, k1, n1, k2, n2, n3, out_0, out_1, out_2
):
    nc = tc.nc
    with ExitStack() as ctx:
        keep = ctx.enter_context(tc.tile_pool(name="keep", bufs=1))
        psum = ctx.enter_context(tc.psum_pool(name="psum", bufs=1))

        def sbuf(name, shape, dtype, tag=""):
            return keep.tile(shape, dtype, name=name, tag=tag, align_bytes=64)

        def load_list(name, dram):
            tile = sbuf(name, list(dram.shape), U16)
            nc.sync.dma_start(tile[:], dram)
            return tile

        def move_scale_rows(dst, src, queues):
            for a in range(PACK):
                queues[a].dma_start(dst[a:P:32, :].bitcast(I32), src[8 * a : P : 32, :].bitcast(I32))

        d_bytes = sbuf("d_bytes", [P, G], U8)
        x_bytes = sbuf("x_bytes", [P, T], U8)
        placed1 = sbuf("placed1", [P, H + S], U8, tag="placed1_then_words2")
        placed2 = sbuf("placed2", [P, H], U8, tag="placed2_then_z")
        nc.gpsimd.memset(x_bytes[:].bitcast(I32), 0)
        nc.vector.memset(d_bytes[:].bitcast(I32), 0)
        nc.vector.memset(placed1[:].bitcast(I32), 0)
        nc.vector.memset(placed2[:].bitcast(I32), 0)

        warm = sbuf("warm", [P, 2], F32)
        nc.gpsimd.memset(warm[:, 0:1], 1.0)
        nc.scalar.activation(warm[:, 1:2], warm[:, 0:1], ACT.Sqrt)

        d_table = sbuf("d_table", [P, G], U32)
        x_table = sbuf("x_table", [P, T], U32)
        d_rows = d_words[0].rearrange("p c r -> p (c r)").bitcast(I32)
        offs_list = load_list("offs_list", offs)
        k1_list = load_list("k1_list", k1)
        nc.sync.dma_start(d_table[:, :LEAD].bitcast(I32), d_rows[:, :LEAD])
        nc.sync.dma_start(x_bytes[0:P:8, :].bitcast(I32), x_scales[0].bitcast(I32))
        nc.sync.dma_start(d_bytes[0:P:8, :].bitcast(I32), d_scales[0].bitcast(I32))
        nc.sync.dma_start(d_table[:, LEAD:].bitcast(I32), d_rows[:, LEAD:])
        k2_list = load_list("k2_list", k2)
        n1_list = load_list("n1_list", n1)
        nc.sync.dma_start(x_table[:].bitcast(I32), x_words[0].rearrange("p c r -> p (c r)").bitcast(I32))
        n2_list = load_list("n2_list", n2)
        n3_list = load_list("n3_list", n3)
        gain = sbuf("gain", [P, PACK], F32)
        nc.gpsimd.dma_start(gain[:], gs.rearrange("(p t) o -> p (t o)", t=PACK))

        picked_bytes1 = sbuf("picked_bytes1", [P, H + S], U8, tag="bytes1_words1_bytes2")
        nc.vector.tensor_copy(picked_bytes1[:, H:], x_bytes[:].indirect(offs_list[:]))
        nc.vector.tensor_copy(picked_bytes1[:, :H], d_bytes[:].indirect(k1_list[:]))
        move_scale_rows(placed1, picked_bytes1, [nc.sync, nc.scalar, nc.sync, nc.scalar])

        picked_words1 = sbuf("picked_words1", [P, H], U32)
        x_picked = sbuf("x_picked", [P, S], U32)
        nc.vector.tensor_copy(picked_words1[:], d_table[:].indirect(k1_list[:]))
        nc.vector.tensor_copy(x_picked[:], x_table[:].indirect(offs_list[:]))

        def deal(dst, src, line, first, count):
            nc.vector.tensor_copy(
                dst.rearrange("p (t c i) -> p c t i", t=count, i=line),
                src.rearrange("p (c i t) -> p c t i", t=PACK, i=line)[:, :, first : first + count, :],
            )

        words1_first = sbuf("words1_first", [P, P], U32)
        bytes1 = sbuf("bytes1", [P, H], U8, tag="dealt_bytes1_then_z_rows")
        deal(words1_first[:], picked_words1[:], 4, 0, 1)
        deal(bytes1[:, :P], placed1[:, :H], 16, 0, 1)

        def product(name, tag, words, scale_bytes, moving, moving_bytes):
            bank = psum.tile([P, moving.shape[1]], F32, name=name, tag=tag)
            nc.tensor.matmul_mx(
                out=bank[:],
                lhsT=words.bitcast(FP8X4),
                lhsT_scale=scale_bytes,
                rhs=moving.bitcast(FP8X4),
                rhs_scale=moving_bytes,
                start=True,
                stop=True,
            )
            return bank

        hidden = [sbuf("hidden%d" % t, [P, S], F32) for t in range(PACK)]
        sent = []

        banks = {}
        halves = [slice(0, HALF), slice(HALF, S)]
        x_plane = placed1[:, H:]

        def first_product(t, words):
            banks[t] = product("first%d" % t, "bank%d" % t, words, bytes1[:, t * P : (t + 1) * P], x_picked[:], x_plane)

        def weigh(t, bank, cols):
            nc.vector.tensor_scalar(hidden[t][:, cols], bank[:], gain[:, t : t + 1], SIXTEENTH, ALU.mult, ALU.mult)

        def send(t):
            sent.append(sbuf("sent%d" % t, [P, 2 * S], F32, tag="sent%d" % t))
            nc.scalar.activation(sent[t][:].indirect(n1_list[:]), hidden[t][:], ACT.Copy)

        def first_layer(t):
            weigh(t, banks[t], slice(0, S))
            send(t)

        for u in range(2):
            bank = product("first0_%d" % u, "bank%d" % (PACK + u), words1_first[:], bytes1[:, :P], x_picked[:, halves[u]], x_plane[:, halves[u]])
            weigh(0, bank, halves[u])
        send(0)
        words1_rest = sbuf("words1_rest", [P, H - P], U32, tag="bytes1_words1_bytes2")
        deal(words1_rest[:], picked_words1[:], 4, 1, PACK - 1)
        deal(bytes1[:, P:], placed1[:, :H], 16, 1, PACK - 1)
        for t in range(1, PACK):
            first_product(t, words1_rest[:, (t - 1) * P : t * P])
        first_layer(1)

        picked_bytes2 = sbuf("picked_bytes2", [P, H], U8, tag="bytes1_words1_bytes2")
        nc.vector.tensor_copy(picked_bytes2[:], d_bytes[:].indirect(k2_list[:]))
        move_scale_rows(placed2, picked_bytes2, [nc.sync] * PACK)
        first_layer(2)
        first_layer(3)

        picked_words2 = sbuf("picked_words2", [P, H], U32, tag="placed1_then_words2")
        nc.vector.tensor_copy(picked_words2[:], d_table[:].indirect(k2_list[:]))
        words2_first = sbuf("words2_first", [P, 2 * P], U32)
        bytes2 = sbuf("bytes2", [P, H], U8)
        z_rows = sbuf("z_rows", [P, PACK - 1, S], BF16, tag="dealt_bytes1_then_z_rows")
        for t in range(PACK - 2):
            nc.vector.tensor_tensor(z_rows[:, t, :], hidden[t][:], sent[t][:, :S], ALU.subtract)
        deal(words2_first[:], picked_words2[:], 4, 0, 2)
        deal(bytes2[:], placed2[:], 16, 0, PACK)
        t = PACK - 2
        nc.vector.tensor_tensor(z_rows[:, t, :], hidden[t][:], sent[t][:, :S], ALU.subtract)

        z_tile = sbuf("z_tile", [P, S * PACK], BF16, tag="placed2_then_z")
        z_flat = [z_tile[:, u * HALF * PACK : (u + 1) * HALF * PACK] for u in range(2)]
        z_grouped = [z_flat[u].rearrange("p (c t) -> p c t", t=PACK) for u in range(2)]
        for u in range(2):
            nc.vector.tensor_copy(z_grouped[u][:, :, : PACK - 1], z_rows[:, :, halves[u]].rearrange("p t c -> p c t"))
        t = PACK - 1
        for u in range(2):
            nc.vector.tensor_tensor(z_grouped[u][:, :, t], hidden[t][:, halves[u]], sent[t][:, halves[u]], ALU.subtract)
        z_words = sbuf("z_words", [P, S], U32)
        z_bytes = sbuf("z_bytes", [P, S], U8)
        for u in range(2):
            nc.vector.quantize_mx(
                out=z_words[:, halves[u]].bitcast(FP8X4),
                scales=z_bytes[:, halves[u]],
                in_=z_flat[u],
            )

        words2_rest = sbuf("words2_rest", [P, 2 * P], U32, tag="sent%d" % (PACK - 1))
        deal(words2_rest[:], picked_words2[:], 4, 2, 2)
        words2 = [tile[:, c * P : (c + 1) * P] for tile in (words2_first, words2_rest) for c in range(2)]

        pairs, rb, radicand, ra, result = [], [], [], [], []
        out_rows = out_0.rearrange("(p t) s -> p t s", t=PACK)

        def fetch(t):
            h2 = sbuf("h2_%d" % t, [P, S], F32)
            if t == 0:
                for u in range(2):
                    bank = product("second0_%d" % u, "bank%d" % (PACK + u), words2[0], bytes2[:, :P], z_words[:, halves[u]], z_bytes[:, halves[u]])
                    nc.scalar.activation(h2[:, halves[u]], bank[:], ACT.Copy, scale=SIXTEENTH)
            else:
                bank = product("second%d" % t, "bank%d" % t, words2[t], bytes2[:, t * P : (t + 1) * P], z_words[:], z_bytes[:])
                nc.vector.tensor_scalar(h2[:], bank[:], SIXTEENTH, None, ALU.mult)
            pairs.append(sbuf("pairs%d" % t, [P, 2 * W], F32, tag="pairs%d" % t))
            nc.scalar.activation(pairs[t][:, :W], h2[:].indirect(n2_list[:]), ACT.Copy)
            nc.scalar.activation(pairs[t][:, W:], h2[:].indirect(n3_list[:]), ACT.Copy)

        def combine(t):
            rb.append(sbuf("rb%d" % t, [P, W], F32))
            nc.vector.scalar_tensor_tensor(rb[t][:], pairs[t][:, :W], -0.5, pairs[t][:, W:], ALU.mult, ALU.add)
            squares = sbuf("squares%d" % t, [P, 2 * W], F32, tag="squares%d" % t)
            nc.vector.tensor_tensor(squares[:], pairs[t][:], pairs[t][:], ALU.mult)
            radicand.append(sbuf("radicand%d" % t, [P, W], F32))
            nc.vector.scalar_tensor_tensor(radicand[t][:], squares[:, :W], 0.25, squares[:, W:], ALU.add, ALU.add)

        def put_rb(t):
            result.append(sbuf("result%d" % t, [P, S], F32))
            nc.scalar.activation(result[t][:].indirect(n3_list[:]), rb[t][:], ACT.Copy)

        def root(t):
            ra.append(sbuf("ra%d" % t, [P, W], F32))
            nc.scalar.activation(ra[t][:], radicand[t][:], ACT.Sqrt)

        def put_ra(t):
            nc.scalar.activation(result[t][:].indirect(n2_list[:]), ra[t][:], ACT.Copy)
            nc.sync.dma_start(out_rows[:, t, :], result[t][:])

        fetch(0)
        fetch(1)
        combine(0)
        put_rb(0)
        root(0)
        fetch(2)
        combine(1)
        put_ra(0)
        root(1)
        put_rb(1)
        fetch(3)
        combine(2)
        put_ra(1)
        root(2)
        put_rb(2)
        combine(3)
        root(3)
        put_rb(3)
        put_ra(2)
        put_ra(3)

        reused = ["pairs%d" % (PACK - 1), "squares%d" % (PACK - 1)]
        out_grouped = [sbuf("out_grouped%d" % u, [P, HALF, PACK], BF16, tag=reused[u]) for u in range(2)]
        for t in range(PACK):
            for u in range(2):
                nc.vector.tensor_copy(out_grouped[u][:, :, t], result[t][:, halves[u]])

        word_rows = out_1[0].rearrange("p c r -> p (c r)").bitcast(I32)
        out_words = sbuf("out_words", [P, S], U32)
        out_bytes = sbuf("out_bytes", [P, S], U8)
        for u in range(2):
            nc.vector.quantize_mx(
                out=out_words[:, halves[u]].bitcast(FP8X4),
                scales=out_bytes[:, halves[u]],
                in_=out_grouped[u][:].rearrange("p c t -> p (c t)"),
            )
            nc.sync.dma_start(word_rows[:, halves[u]], out_words[:, halves[u]].bitcast(I32))
        scale_rows = out_2[0].bitcast(I32)
        for q in range(4):
            queue = nc.scalar if q % 2 == 0 else nc.sync
            queue.dma_start(scale_rows[4 * q : 4 * q + 4, :], out_bytes[32 * q : 32 * q + 4, :].bitcast(I32))
